import numpy as np, ml_dtypes
CORES = [3,11,19,27,35]
N = 5
MB, TK = 8, 128
def setup_inputs(rng):
    return {"x": rng.standard_normal((N, MB, 128, TK), dtype=np.float32).astype(ml_dtypes.bfloat16), "w": (rng.standard_normal((N, 128, 128), dtype=np.float32) / 8).astype(ml_dtypes.bfloat16)}
def reference(x, w):
    def run(a, W, order):
        for s in order:
            a = np.maximum(np.einsum("kf,bkn->bfn", W[s].astype(np.float64), a), 0.0)
        return a
    dt = ml_dtypes.bfloat16 if x.dtype != np.float64 else np.float64
    y = np.full(x.shape, np.nan, dt)
    y[N - 1] = run(x[0].astype(np.float64), w, range(N)).astype(dt)
    return {"y": y}

@@ -1,0 +1,103 @@
+from concourse.mybir import AluOpType
+
+N, MB, TK = 5, 8, 128
+CHUNKS = (2, 2, 2, 2)
+assert sum(CHUNKS) == MB
+NCH = len(CHUNKS)
+
+SCRATCH = {
+    "xs": ("sbuf", [128, MB * TK], "bfloat16"),
+    "wb": ("sbuf", [128, N * 128], "bfloat16"),
+    "zero": ("sbuf", [128, TK], "float32"),
+}
+for _l in range(1, N + 1):
+    SCRATCH["a%d" % _l] = ("sbuf", [128, MB * TK], "bfloat16")
+for _u in range(MB):
+    SCRATCH["ps%d" % _u] = ("psum", [128, 512], "float32")
+
+SEMAPHORES = (["wld", "zs", "sent", "stored"]
+              + ["xld%d" % m for m in range(MB)]
+              + ["mm%d" % m for m in range(MB)]
+              + ["rl%d" % m for m in range(MB)]
+              + ["rdy%d" % c for c in range(NCH)]
+              + ["arr%d" % c for c in range(NCH)]
+              + ["warr%d" % s for s in range(N)])
+
+
+def _cols(m, n=1):
+    return slice(m * TK, (m + n) * TK)
+
+
+def _send(g, topo, src, dst, ap_out, ap_in, remote_sem, local_sem):
+    assert topo.may_write(src, dst)
+    rid, pid, _ = topo.addr(dst)
+    mask = topo.mask(src, dst)
+    g.remote_dma(ap_out, ap_in, remote_sem, local_sem, pid, rid, mask)
+    return bin(mask).count("1")
+
+
+def rank_program(g, core, T, topo):
+    rank = T.rank_of(core)
+    if rank is None:
+        return
+    sem = T.sem
+    last = T.cores[N - 1]
+    starts = [sum(CHUNKS[:c]) for c in range(NCH)]
+    wcol = slice(rank * 128, (rank + 1) * 128)
+
+    g.sync.dma_start(T.wb[:, wcol], T.w[:]).then_inc(sem.wld, 16)
+
+    if 0 < rank < N - 1:
+        g.wait_ge(sem.wld, 16)
+        n = _send(g, topo, core, last, T.wb[:, wcol], T.wb[:, wcol], sem["warr%d" % rank], sem.sent)
+        g.wait_ge(sem.sent, n)
+        return
+
+    g.vector.memset(T.zero[:], 0.0).then_inc(sem.zs, 1)
+    g.vector.wait_ge(sem.zs, 1)
+
+    if rank == 0:
+        for m in range(MB):
+            q = (g.scalar, g.sync)[m % 2]
+            q.dma_start(T.xs[:, _cols(m)], T.x[m]).then_inc(sem["xld%d" % m], 16)
+        g.tensor.wait_ge(sem.wld, 16)
+        total = 0
+        for c in range(NCH):
+            for m in range(starts[c], starts[c] + CHUNKS[c]):
+                ps = T["ps%d" % m][:, 0:TK]
+                g.tensor.wait_ge(sem["xld%d" % m], 16)
+                g.tensor.matmul(ps, T.wb[:, wcol], T.xs[:, _cols(m)], True, True).then_inc(sem["mm%d" % m], 1)
+                g.vector.wait_ge(sem["mm%d" % m], 1)
+                g.vector.tensor_tensor(T.a1[:, _cols(m)], ps, T.zero[:], AluOpType.max).then_inc(sem["rdy%d" % c], 1)
+            g.wait_ge(sem["rdy%d" % c], CHUNKS[c])
+            blk = _cols(starts[c], CHUNKS[c])
+            total += _send(g, topo, core, last, T.a1[:, blk], T.a1[:, blk], sem["arr%d" % c], sem.sent)
+        g.wait_ge(sem.sent, total)
+        return
+
+    first = T.cores[0]
+    have_w = set()
+    for c in range(NCH):
+        units = range(starts[c], starts[c] + CHUNKS[c])
+        g.tensor.wait_ge(sem["arr%d" % c], bin(topo.mask(first, core)).count("1"))
+        for l in range(1, N):
+            if l not in have_w:
+                have_w.add(l)
+                if l == rank:
+                    g.tensor.wait_ge(sem.wld, 16)
+                else:
+                    g.tensor.wait_ge(sem["warr%d" % l], bin(topo.mask(T.cores[l], core)).count("1"))
+            for u in units:
+                ps = T["ps%d" % u][:, 0:TK]
+                if l > 1:
+                    g.tensor.wait_ge(sem["rl%d" % u], l - 1)
+                g.tensor.matmul(ps, T.wb[:, l * 128:(l + 1) * 128], T["a%d" % l][:, _cols(u)], True, True
+                                ).then_inc(sem["mm%d" % u], 1)
+                g.vector.wait_ge(sem["mm%d" % u], l)
+                g.vector.tensor_tensor(T["a%d" % (l + 1)][:, _cols(u)], ps, T.zero[:], AluOpType.max
+                                       ).then_inc(sem["rl%d" % u], 1)
+        for u in units:
+            q = (g.sync, g.scalar)[u % 2]
+            q.wait_ge(sem["rl%d" % u], N - 1)
+            q.dma_start(T.y[u], T["a%d" % N][:, _cols(u)]).then_inc(sem.stored, 16)
+    g.wait_ge(sem.stored, 16 * MB)

@@ -1,12 +1,13 @@
 from concourse.mybir import AluOpType
 
 N, MB, TK = 5, 8, 128
-CHUNKS = (2, 2, 2, 2)
-assert sum(CHUNKS) == MB
+CHUNKS = (2, 2, 2)
+KEEP = 2
+assert sum(CHUNKS) + KEEP == MB
 NCH = len(CHUNKS)
 
 SCRATCH = {
-    "xs": ("sbuf", [128, MB * TK], "bfloat16"),
+    "a0": ("sbuf", [128, MB * TK], "bfloat16"),
     "wb": ("sbuf", [128, N * 128], "bfloat16"),
     "zero": ("sbuf", [128, TK], "float32"),
 }
@@ -15,11 +16,10 @@ for _l in range(1, N + 1):
 for _u in range(MB):
     SCRATCH["ps%d" % _u] = ("psum", [128, 512], "float32")
 
-SEMAPHORES = (["wld", "zs", "sent", "stored"]
+SEMAPHORES = (["wld", "zs", "sent", "stored", "fin"]
               + ["xld%d" % m for m in range(MB)]
               + ["mm%d" % m for m in range(MB)]
               + ["rl%d" % m for m in range(MB)]
-              + ["rdy%d" % c for c in range(NCH)]
               + ["arr%d" % c for c in range(NCH)]
               + ["warr%d" % s for s in range(N)])
 
@@ -28,12 +28,15 @@ def _cols(m, n=1):
     return slice(m * TK, (m + n) * TK)
 
 
-def _send(g, topo, src, dst, ap_out, ap_in, remote_sem, local_sem):
+def _engines(topo, src, dst):
+    return bin(topo.mask(src, dst)).count("1")
+
+
+def _send(g, topo, src, dst, ap, remote_sem, local_sem):
     assert topo.may_write(src, dst)
     rid, pid, _ = topo.addr(dst)
-    mask = topo.mask(src, dst)
-    g.remote_dma(ap_out, ap_in, remote_sem, local_sem, pid, rid, mask)
-    return bin(mask).count("1")
+    g.remote_dma(ap, ap, remote_sem, local_sem, pid, rid, topo.mask(src, dst))
+    return _engines(topo, src, dst)
 
 
 def rank_program(g, core, T, topo):
@@ -41,63 +44,82 @@ def rank_program(g, core, T, topo):
     if rank is None:
         return
     sem = T.sem
-    last = T.cores[N - 1]
+    first, last = T.cores[0], T.cores[N - 1]
     starts = [sum(CHUNKS[:c]) for c in range(NCH)]
+    kept = range(MB - KEEP, MB)
     wcol = slice(rank * 128, (rank + 1) * 128)
 
     g.sync.dma_start(T.wb[:, wcol], T.w[:]).then_inc(sem.wld, 16)
 
     if 0 < rank < N - 1:
         g.wait_ge(sem.wld, 16)
-        n = _send(g, topo, core, last, T.wb[:, wcol], T.wb[:, wcol], sem["warr%d" % rank], sem.sent)
+        n = _send(g, topo, core, first, T.wb[:, wcol], sem["warr%d" % rank], sem.sent)
+        n += _send(g, topo, core, last, T.wb[:, wcol], sem["warr%d" % rank], sem.sent)
         g.wait_ge(sem.sent, n)
         return
 
     g.vector.memset(T.zero[:], 0.0).then_inc(sem.zs, 1)
     g.vector.wait_ge(sem.zs, 1)
-
-    if rank == 0:
-        for m in range(MB):
-            q = (g.scalar, g.sync)[m % 2]
-            q.dma_start(T.xs[:, _cols(m)], T.x[m]).then_inc(sem["xld%d" % m], 16)
-        g.tensor.wait_ge(sem.wld, 16)
-        total = 0
-        for c in range(NCH):
-            for m in range(starts[c], starts[c] + CHUNKS[c]):
-                ps = T["ps%d" % m][:, 0:TK]
-                g.tensor.wait_ge(sem["xld%d" % m], 16)
-                g.tensor.matmul(ps, T.wb[:, wcol], T.xs[:, _cols(m)], True, True).then_inc(sem["mm%d" % m], 1)
-                g.vector.wait_ge(sem["mm%d" % m], 1)
-                g.vector.tensor_tensor(T.a1[:, _cols(m)], ps, T.zero[:], AluOpType.max).then_inc(sem["rdy%d" % c], 1)
-            g.wait_ge(sem["rdy%d" % c], CHUNKS[c])
-            blk = _cols(starts[c], CHUNKS[c])
-            total += _send(g, topo, core, last, T.a1[:, blk], T.a1[:, blk], sem["arr%d" % c], sem.sent)
-        g.wait_ge(sem.sent, total)
-        return
-
-    first = T.cores[0]
     have_w = set()
-    for c in range(NCH):
-        units = range(starts[c], starts[c] + CHUNKS[c])
-        g.tensor.wait_ge(sem["arr%d" % c], bin(topo.mask(first, core)).count("1"))
-        for l in range(1, N):
+
+    def run(units, l0, l1, ready):
+        for l in range(l0, l1):
             if l not in have_w:
                 have_w.add(l)
                 if l == rank:
                     g.tensor.wait_ge(sem.wld, 16)
                 else:
-                    g.tensor.wait_ge(sem["warr%d" % l], bin(topo.mask(T.cores[l], core)).count("1"))
+                    g.tensor.wait_ge(sem["warr%d" % l], _engines(topo, T.cores[l], core))
             for u in units:
                 ps = T["ps%d" % u][:, 0:TK]
-                if l > 1:
-                    g.tensor.wait_ge(sem["rl%d" % u], l - 1)
+                if l == l0:
+                    ready(u)
+                else:
+                    g.tensor.wait_ge(sem["rl%d" % u], l - l0)
                 g.tensor.matmul(ps, T.wb[:, l * 128:(l + 1) * 128], T["a%d" % l][:, _cols(u)], True, True
                                 ).then_inc(sem["mm%d" % u], 1)
-                g.vector.wait_ge(sem["mm%d" % u], l)
+                g.vector.wait_ge(sem["mm%d" % u], l - l0 + 1)
                 g.vector.tensor_tensor(T["a%d" % (l + 1)][:, _cols(u)], ps, T.zero[:], AluOpType.max
                                        ).then_inc(sem["rl%d" % u], 1)
+
+    if rank == 0:
+        for m in range(MB):
+            q = (g.scalar, g.sync)[m % 2]
+            q.dma_start(T.a0[:, _cols(m)], T.x[m]).then_inc(sem["xld%d" % m], 16)
+
+        def loaded(u):
+            g.tensor.wait_ge(sem["xld%d" % u], 16)
+
+        total = 0
+        for c in range(NCH):
+            units = range(starts[c], starts[c] + CHUNKS[c])
+            run(units, 0, 1, loaded)
+            for u in units:
+                g.wait_ge(sem["rl%d" % u], 1)
+            total += _send(g, topo, core, last, T.a1[:, _cols(starts[c], CHUNKS[c])], sem["arr%d" % c], sem.sent)
+        run(kept, 0, N, loaded)
+        for u in kept:
+            g.wait_ge(sem["rl%d" % u], N)
+        total += _send(g, topo, core, last, T["a%d" % N][:, _cols(MB - KEEP, KEEP)], sem.fin, sem.sent)
+        g.wait_ge(sem.sent, total)
+        return
+
+    g.wait_ge(sem.wld, 16)
+    total = _send(g, topo, core, first, T.wb[:, wcol], sem["warr%d" % rank], sem.sent)
+
+    def store(u):
+        q = (g.sync, g.scalar)[u % 2]
+        q.dma_start(T.y[u], T["a%d" % N][:, _cols(u)]).then_inc(sem.stored, 16)
+
+    for c in range(NCH):
+        units = range(starts[c], starts[c] + CHUNKS[c])
+        g.tensor.wait_ge(sem["arr%d" % c], _engines(topo, first, core))
+        run(units, 1, N, lambda u: None)
         for u in units:
-            q = (g.sync, g.scalar)[u % 2]
-            q.wait_ge(sem["rl%d" % u], N - 1)
-            q.dma_start(T.y[u], T["a%d" % N][:, _cols(u)]).then_inc(sem.stored, 16)
+            (g.sync, g.scalar)[u % 2].wait_ge(sem["rl%d" % u], N - 1)
+            store(u)
+    for u in kept:
+        (g.sync, g.scalar)[u % 2].wait_ge(sem.fin, _engines(topo, first, core))
+        store(u)
+    g.wait_ge(sem.sent, total)
     g.wait_ge(sem.stored, 16 * MB)

@@ -3,13 +3,15 @@ from concourse.mybir import AluOpType
 N, MB, TK = 5, 8, 128
 CHUNKS = (2, 2, 2)
 KEEP = 2
+GROUPS = (((0, 1), (1, 1)), ((2, 2), (4, 2)))
+WIDEST = 2
 assert sum(CHUNKS) + KEEP == MB
 NCH = len(CHUNKS)
 
 SCRATCH = {
     "a0": ("sbuf", [128, MB * TK], "bfloat16"),
     "wb": ("sbuf", [128, N * 128], "bfloat16"),
-    "zero": ("sbuf", [128, TK], "float32"),
+    "zero": ("sbuf", [128, WIDEST * TK], "float32"),
 }
 for _l in range(1, N + 1):
     SCRATCH["a%d" % _l] = ("sbuf", [128, MB * TK], "bfloat16")
@@ -46,7 +48,6 @@ def rank_program(g, core, T, topo):
     sem = T.sem
     first, last = T.cores[0], T.cores[N - 1]
     starts = [sum(CHUNKS[:c]) for c in range(NCH)]
-    kept = range(MB - KEEP, MB)
     wcol = slice(rank * 128, (rank + 1) * 128)
 
     g.sync.dma_start(T.wb[:, wcol], T.w[:]).then_inc(sem.wld, 16)
@@ -70,56 +71,63 @@ def rank_program(g, core, T, topo):
                     g.tensor.wait_ge(sem.wld, 16)
                 else:
                     g.tensor.wait_ge(sem["warr%d" % l], _engines(topo, T.cores[l], core))
-            for u in units:
-                ps = T["ps%d" % u][:, 0:TK]
+            for m0, n in units:
+                ps = T["ps%d" % m0][:, 0:n * TK]
                 if l == l0:
-                    ready(u)
+                    for m in range(m0, m0 + n):
+                        ready(m)
                 else:
-                    g.tensor.wait_ge(sem["rl%d" % u], l - l0)
-                g.tensor.matmul(ps, T.wb[:, l * 128:(l + 1) * 128], T["a%d" % l][:, _cols(u)], True, True
-                                ).then_inc(sem["mm%d" % u], 1)
-                g.vector.wait_ge(sem["mm%d" % u], l - l0 + 1)
-                g.vector.tensor_tensor(T["a%d" % (l + 1)][:, _cols(u)], ps, T.zero[:], AluOpType.max
-                                       ).then_inc(sem["rl%d" % u], 1)
+                    g.tensor.wait_ge(sem["rl%d" % m0], l - l0)
+                g.tensor.matmul(ps, T.wb[:, l * 128:(l + 1) * 128], T["a%d" % l][:, _cols(m0, n)], True, True
+                                ).then_inc(sem["mm%d" % m0], 1)
+                g.vector.wait_ge(sem["mm%d" % m0], l - l0 + 1)
+                g.vector.tensor_tensor(T["a%d" % (l + 1)][:, _cols(m0, n)], ps, T.zero[:, 0:n * TK], AluOpType.max
+                                       ).then_inc(sem["rl%d" % m0], 1)
 
     if rank == 0:
         for m in range(MB):
             q = (g.scalar, g.sync)[m % 2]
             q.dma_start(T.a0[:, _cols(m)], T.x[m]).then_inc(sem["xld%d" % m], 16)
 
-        def loaded(u):
-            g.tensor.wait_ge(sem["xld%d" % u], 16)
+        def loaded(m):
+            g.tensor.wait_ge(sem["xld%d" % m], 16)
 
         total = 0
         for c in range(NCH):
-            units = range(starts[c], starts[c] + CHUNKS[c])
+            units = [(m, 1) for m in range(starts[c], starts[c] + CHUNKS[c])]
             run(units, 0, 1, loaded)
-            for u in units:
-                g.wait_ge(sem["rl%d" % u], 1)
+            for m, _ in units:
+                g.wait_ge(sem["rl%d" % m], 1)
             total += _send(g, topo, core, last, T.a1[:, _cols(starts[c], CHUNKS[c])], sem["arr%d" % c], sem.sent)
+        kept = [(m, 1) for m in range(MB - KEEP, MB)]
         run(kept, 0, N, loaded)
-        for u in kept:
-            g.wait_ge(sem["rl%d" % u], N)
+        for m, _ in kept:
+            g.wait_ge(sem["rl%d" % m], N)
         total += _send(g, topo, core, last, T["a%d" % N][:, _cols(MB - KEEP, KEEP)], sem.fin, sem.sent)
         g.wait_ge(sem.sent, total)
         return
 
     g.wait_ge(sem.wld, 16)
     total = _send(g, topo, core, first, T.wb[:, wcol], sem["warr%d" % rank], sem.sent)
+    seen = set()
 
-    def store(u):
-        q = (g.sync, g.scalar)[u % 2]
-        q.dma_start(T.y[u], T["a%d" % N][:, _cols(u)]).then_inc(sem.stored, 16)
+    def landed(m):
+        c = max(c for c in range(NCH) if starts[c] <= m)
+        if c not in seen:
+            seen.add(c)
+            g.tensor.wait_ge(sem["arr%d" % c], _engines(topo, first, core))
 
-    for c in range(NCH):
-        units = range(starts[c], starts[c] + CHUNKS[c])
-        g.tensor.wait_ge(sem["arr%d" % c], _engines(topo, first, core))
-        run(units, 1, N, lambda u: None)
-        for u in units:
-            (g.sync, g.scalar)[u % 2].wait_ge(sem["rl%d" % u], N - 1)
-            store(u)
-    for u in kept:
-        (g.sync, g.scalar)[u % 2].wait_ge(sem.fin, _engines(topo, first, core))
-        store(u)
+    def store(m, s, v):
+        q = (g.sync, g.scalar)[m % 2]
+        q.wait_ge(s, v)
+        q.dma_start(T.y[m], T["a%d" % N][:, _cols(m)]).then_inc(sem.stored, 16)
+
+    for units in GROUPS:
+        run(units, 1, N, landed)
+        for m0, n in units:
+            for m in range(m0, m0 + n):
+                store(m, sem["rl%d" % m0], N - 1)
+    for m in range(MB - KEEP, MB):
+        store(m, sem.fin, _engines(topo, first, core))
     g.wait_ge(sem.sent, total)
     g.wait_ge(sem.stored, 16 * MB)

@@ -3,13 +3,16 @@ from concourse.mybir import AluOpType
 N, MB, TK = 5, 8, 128
 CHUNKS = (2, 2, 2)
 KEEP = 2
-GROUPS = (((0, 1), (1, 1)), ((2, 2), (4, 2)))
+GROUPS = (((0, 2), (2, 2), (4, 2)),)
+SKEW = True
 WIDEST = 2
+FIN_ENGINES = None
 assert sum(CHUNKS) + KEEP == MB
 NCH = len(CHUNKS)
 
 SCRATCH = {
     "a0": ("sbuf", [128, MB * TK], "bfloat16"),
+    "w0": ("sbuf", [128, 2 * 128], "bfloat16"),
     "wb": ("sbuf", [128, N * 128], "bfloat16"),
     "zero": ("sbuf", [128, WIDEST * TK], "float32"),
 }
@@ -30,15 +33,29 @@ def _cols(m, n=1):
     return slice(m * TK, (m + n) * TK)
 
 
-def _engines(topo, src, dst):
-    return bin(topo.mask(src, dst)).count("1")
+def _mask(topo, src, dst, limit=None):
+    bits = [b for b in range(16) if topo.mask(src, dst) >> b & 1]
+    return sum(1 << b for b in bits[:limit])
 
 
-def _send(g, topo, src, dst, ap, remote_sem, local_sem):
+def _engines(topo, src, dst, limit=None):
+    return bin(_mask(topo, src, dst, limit)).count("1")
+
+
+def _send(g, topo, src, dst, ap, remote_sem, local_sem, limit=None):
     assert topo.may_write(src, dst)
     rid, pid, _ = topo.addr(dst)
-    g.remote_dma(ap, ap, remote_sem, local_sem, pid, rid, topo.mask(src, dst))
-    return _engines(topo, src, dst)
+    g.remote_dma(ap, ap, remote_sem, local_sem, pid, rid, _mask(topo, src, dst, limit))
+    return _engines(topo, src, dst, limit)
+
+
+def _by_layer(units, l0, l1):
+    return [(u, l) for l in range(l0, l1) for u in units]
+
+
+def _skewed(units, l0, l1):
+    return [(u, l0 + d - j) for d in range(len(units) + l1 - l0 - 1) for j, u in enumerate(units)
+            if 0 <= d - j < l1 - l0]
 
 
 def rank_program(g, core, T, topo):
@@ -50,11 +67,19 @@ def rank_program(g, core, T, topo):
     starts = [sum(CHUNKS[:c]) for c in range(NCH)]
     wcol = slice(rank * 128, (rank + 1) * 128)
 
-    g.sync.dma_start(T.wb[:, wcol], T.w[:]).then_inc(sem.wld, 16)
+    if rank == 0:
+        g.sync.dma_start(T.w0[0:64, :], T.w[:]).then_inc(sem.wld, 16)
+        g.scalar.dma_start(T.w0[64:128, :], T.w[:]).then_inc(sem.wld, 16)
+        wld = 32
+    else:
+        g.sync.dma_start(T.wb[:, wcol], T.w[:]).then_inc(sem.wld, 16)
+        wld = 16
 
     if 0 < rank < N - 1:
-        g.wait_ge(sem.wld, 16)
-        n = _send(g, topo, core, first, T.wb[:, wcol], sem["warr%d" % rank], sem.sent)
+        g.wait_ge(sem.wld, wld)
+        n = 0
+        if KEEP:
+            n += _send(g, topo, core, first, T.wb[:, wcol], sem["warr%d" % rank], sem.sent)
         n += _send(g, topo, core, last, T.wb[:, wcol], sem["warr%d" % rank], sem.sent)
         g.wait_ge(sem.sent, n)
         return
@@ -63,31 +88,37 @@ def rank_program(g, core, T, topo):
     g.vector.wait_ge(sem.zs, 1)
     have_w = set()
 
-    def run(units, l0, l1, ready):
-        for l in range(l0, l1):
+    def run(seq, l0, ready):
+        for (m0, n), l in seq:
             if l not in have_w:
                 have_w.add(l)
                 if l == rank:
-                    g.tensor.wait_ge(sem.wld, 16)
+                    g.tensor.wait_ge(sem.wld, wld)
                 else:
                     g.tensor.wait_ge(sem["warr%d" % l], _engines(topo, T.cores[l], core))
-            for m0, n in units:
-                ps = T["ps%d" % m0][:, 0:n * TK]
-                if l == l0:
-                    for m in range(m0, m0 + n):
-                        ready(m)
-                else:
-                    g.tensor.wait_ge(sem["rl%d" % m0], l - l0)
-                g.tensor.matmul(ps, T.wb[:, l * 128:(l + 1) * 128], T["a%d" % l][:, _cols(m0, n)], True, True
-                                ).then_inc(sem["mm%d" % m0], 1)
-                g.vector.wait_ge(sem["mm%d" % m0], l - l0 + 1)
-                g.vector.tensor_tensor(T["a%d" % (l + 1)][:, _cols(m0, n)], ps, T.zero[:, 0:n * TK], AluOpType.max
-                                       ).then_inc(sem["rl%d" % m0], 1)
+            ps = T["ps%d" % m0][:, 0:n * TK]
+            if l == l0:
+                for m in range(m0, m0 + n):
+                    ready(m)
+            else:
+                g.tensor.wait_ge(sem["rl%d" % m0], l - l0)
+            if l == 0:
+                assert n == 1
+                half = slice(64 * (m0 % 2), 64 * (m0 % 2) + 64)
+                g.tensor.matmul(ps, T.w0[half, 0:128], T.a0[half, _cols(m0 // 2 * 2)], True, False)
+                mm = g.tensor.matmul(ps, T.w0[half, 128:256], T.a0[half, _cols(m0 // 2 * 2 + 1)], False, True)
+            else:
+                mm = g.tensor.matmul(ps, T.wb[:, l * 128:(l + 1) * 128], T["a%d" % l][:, _cols(m0, n)], True, True)
+            mm.then_inc(sem["mm%d" % m0], 1)
+            g.vector.wait_ge(sem["mm%d" % m0], l - l0 + 1)
+            g.vector.tensor_tensor(T["a%d" % (l + 1)][:, _cols(m0, n)], ps, T.zero[:, 0:n * TK], AluOpType.max
+                                   ).then_inc(sem["rl%d" % m0], 1)
 
     if rank == 0:
         for m in range(MB):
-            q = (g.scalar, g.sync)[m % 2]
-            q.dma_start(T.a0[:, _cols(m)], T.x[m]).then_inc(sem["xld%d" % m], 16)
+            q = (g.sync, g.scalar)[m % 2]
+            q.dma_start(T.a0[64 * (m % 2):64 * (m % 2) + 64, _cols(m // 2 * 2, 2)], T.x[m]
+                        ).then_inc(sem["xld%d" % m], 16)
 
         def loaded(m):
             g.tensor.wait_ge(sem["xld%d" % m], 16)
@@ -95,20 +126,24 @@ def rank_program(g, core, T, topo):
         total = 0
         for c in range(NCH):
             units = [(m, 1) for m in range(starts[c], starts[c] + CHUNKS[c])]
-            run(units, 0, 1, loaded)
+            run(_by_layer(units, 0, 1), 0, loaded)
             for m, _ in units:
                 g.wait_ge(sem["rl%d" % m], 1)
             total += _send(g, topo, core, last, T.a1[:, _cols(starts[c], CHUNKS[c])], sem["arr%d" % c], sem.sent)
-        kept = [(m, 1) for m in range(MB - KEEP, MB)]
-        run(kept, 0, N, loaded)
-        for m, _ in kept:
-            g.wait_ge(sem["rl%d" % m], N)
-        total += _send(g, topo, core, last, T["a%d" % N][:, _cols(MB - KEEP, KEEP)], sem.fin, sem.sent)
+        if KEEP:
+            kept = [(m, 1) for m in range(MB - KEEP, MB)]
+            run(_by_layer(kept, 0, N), 0, loaded)
+            for m, _ in kept:
+                g.wait_ge(sem["rl%d" % m], N)
+            total += _send(g, topo, core, last, T["a%d" % N][:, _cols(MB - KEEP, KEEP)], sem.fin, sem.sent,
+                           FIN_ENGINES)
         g.wait_ge(sem.sent, total)
         return
 
-    g.wait_ge(sem.wld, 16)
-    total = _send(g, topo, core, first, T.wb[:, wcol], sem["warr%d" % rank], sem.sent)
+    total = 0
+    if KEEP:
+        g.wait_ge(sem.wld, wld)
+        total = _send(g, topo, core, first, T.wb[:, wcol], sem["warr%d" % rank], sem.sent)
     seen = set()
 
     def landed(m):
@@ -123,11 +158,12 @@ def rank_program(g, core, T, topo):
         q.dma_start(T.y[m], T["a%d" % N][:, _cols(m)]).then_inc(sem.stored, 16)
 
     for units in GROUPS:
-        run(units, 1, N, landed)
+        run((_skewed if SKEW else _by_layer)(units, 1, N), 1, landed)
         for m0, n in units:
             for m in range(m0, m0 + n):
                 store(m, sem["rl%d" % m0], N - 1)
     for m in range(MB - KEEP, MB):
-        store(m, sem.fin, _engines(topo, first, core))
-    g.wait_ge(sem.sent, total)
+        store(m, sem.fin, _engines(topo, first, core, FIN_ENGINES))
+    if total:
+        g.wait_ge(sem.sent, total)
     g.wait_ge(sem.stored, 16 * MB)

from concourse.mybir import AluOpType

N, MB, TK = 5, 8, 128
CHUNKS = (2, 2, 2)
KEEP = 2
GROUPS = (((0, 2), (2, 2), (4, 2)),)
SKEW = True
WIDEST = 2
FIN_ENGINES = None
assert sum(CHUNKS) + KEEP == MB
NCH = len(CHUNKS)

SCRATCH = {
    "a0": ("sbuf", [128, MB * TK], "bfloat16"),
    "w0": ("sbuf", [128, 2 * 128], "bfloat16"),
    "wb": ("sbuf", [128, N * 128], "bfloat16"),
    "zero": ("sbuf", [128, WIDEST * TK], "float32"),
}
for _l in range(1, N + 1):
    SCRATCH["a%d" % _l] = ("sbuf", [128, MB * TK], "bfloat16")
for _u in range(MB):
    SCRATCH["ps%d" % _u] = ("psum", [128, 512], "float32")

SEMAPHORES = (["wld", "zs", "sent", "stored", "fin"]
              + ["xld%d" % m for m in range(MB)]
              + ["mm%d" % m for m in range(MB)]
              + ["rl%d" % m for m in range(MB)]
              + ["arr%d" % c for c in range(NCH)]
              + ["warr%d" % s for s in range(N)])


def _cols(m, n=1):
    return slice(m * TK, (m + n) * TK)


def _mask(topo, src, dst, limit=None):
    bits = [b for b in range(16) if topo.mask(src, dst) >> b & 1]
    return sum(1 << b for b in bits[:limit])


def _engines(topo, src, dst, limit=None):
    return bin(_mask(topo, src, dst, limit)).count("1")


def _send(g, topo, src, dst, ap, remote_sem, local_sem, limit=None):
    assert topo.may_write(src, dst)
    rid, pid, _ = topo.addr(dst)
    g.remote_dma(ap, ap, remote_sem, local_sem, pid, rid, _mask(topo, src, dst, limit))
    return _engines(topo, src, dst, limit)


def _by_layer(units, l0, l1):
    return [(u, l) for l in range(l0, l1) for u in units]


def _skewed(units, l0, l1):
    return [(u, l0 + d - j) for d in range(len(units) + l1 - l0 - 1) for j, u in enumerate(units)
            if 0 <= d - j < l1 - l0]


def rank_program(g, core, T, topo):
    rank = T.rank_of(core)
    if rank is None:
        return
    sem = T.sem
    first, last = T.cores[0], T.cores[N - 1]
    starts = [sum(CHUNKS[:c]) for c in range(NCH)]
    wcol = slice(rank * 128, (rank + 1) * 128)

    if rank == 0:
        g.sync.dma_start(T.w0[0:64, :], T.w[:]).then_inc(sem.wld, 16)
        g.scalar.dma_start(T.w0[64:128, :], T.w[:]).then_inc(sem.wld, 16)
        wld = 32
    else:
        g.sync.dma_start(T.wb[:, wcol], T.w[:]).then_inc(sem.wld, 16)
        wld = 16

    if 0 < rank < N - 1:
        g.wait_ge(sem.wld, wld)
        n = 0
        if KEEP:
            n += _send(g, topo, core, first, T.wb[:, wcol], sem["warr%d" % rank], sem.sent)
        n += _send(g, topo, core, last, T.wb[:, wcol], sem["warr%d" % rank], sem.sent)
        g.wait_ge(sem.sent, n)
        return

    g.vector.memset(T.zero[:], 0.0).then_inc(sem.zs, 1)
    g.vector.wait_ge(sem.zs, 1)
    have_w = set()

    def run(seq, l0, ready):
        for (m0, n), l in seq:
            if l not in have_w:
                have_w.add(l)
                if l == rank:
                    g.tensor.wait_ge(sem.wld, wld)
                else:
                    g.tensor.wait_ge(sem["warr%d" % l], _engines(topo, T.cores[l], core))
            ps = T["ps%d" % m0][:, 0:n * TK]
            if l == l0:
                for m in range(m0, m0 + n):
                    ready(m)
            else:
                g.tensor.wait_ge(sem["rl%d" % m0], l - l0)
            if l == 0:
                assert n == 1
                half = slice(64 * (m0 % 2), 64 * (m0 % 2) + 64)
                g.tensor.matmul(ps, T.w0[half, 0:128], T.a0[half, _cols(m0 // 2 * 2)], True, False)
                mm = g.tensor.matmul(ps, T.w0[half, 128:256], T.a0[half, _cols(m0 // 2 * 2 + 1)], False, True)
            else:
                mm = g.tensor.matmul(ps, T.wb[:, l * 128:(l + 1) * 128], T["a%d" % l][:, _cols(m0, n)], True, True)
            mm.then_inc(sem["mm%d" % m0], 1)
            g.vector.wait_ge(sem["mm%d" % m0], l - l0 + 1)
            g.vector.tensor_tensor(T["a%d" % (l + 1)][:, _cols(m0, n)], ps, T.zero[:, 0:n * TK], AluOpType.max
                                   ).then_inc(sem["rl%d" % m0], 1)

    if rank == 0:
        for m in range(MB):
            q = (g.sync, g.scalar)[m % 2]
            q.dma_start(T.a0[64 * (m % 2):64 * (m % 2) + 64, _cols(m // 2 * 2, 2)], T.x[m]
                        ).then_inc(sem["xld%d" % m], 16)

        def loaded(m):
            g.tensor.wait_ge(sem["xld%d" % m], 16)

        total = 0
        for c in range(NCH):
            units = [(m, 1) for m in range(starts[c], starts[c] + CHUNKS[c])]
            run(_by_layer(units, 0, 1), 0, loaded)
            for m, _ in units:
                g.wait_ge(sem["rl%d" % m], 1)
            total += _send(g, topo, core, last, T.a1[:, _cols(starts[c], CHUNKS[c])], sem["arr%d" % c], sem.sent)
        if KEEP:
            kept = [(m, 1) for m in range(MB - KEEP, MB)]
            run(_by_layer(kept, 0, N), 0, loaded)
            for m, _ in kept:
                g.wait_ge(sem["rl%d" % m], N)
            total += _send(g, topo, core, last, T["a%d" % N][:, _cols(MB - KEEP, KEEP)], sem.fin, sem.sent,
                           FIN_ENGINES)
        g.wait_ge(sem.sent, total)
        return

    total = 0
    if KEEP:
        g.wait_ge(sem.wld, wld)
        total = _send(g, topo, core, first, T.wb[:, wcol], sem["warr%d" % rank], sem.sent)
    seen = set()

    def landed(m):
        c = max(c for c in range(NCH) if starts[c] <= m)
        if c not in seen:
            seen.add(c)
            g.tensor.wait_ge(sem["arr%d" % c], _engines(topo, first, core))

    def store(m, s, v):
        q = (g.sync, g.scalar)[m % 2]
        q.wait_ge(s, v)
        q.dma_start(T.y[m], T["a%d" % N][:, _cols(m)]).then_inc(sem.stored, 16)

    for units in GROUPS:
        run((_skewed if SKEW else _by_layer)(units, 1, N), 1, landed)
        for m0, n in units:
            for m in range(m0, m0 + n):
                store(m, sem["rl%d" % m0], N - 1)
    for m in range(MB - KEEP, MB):
        store(m, sem.fin, _engines(topo, first, core, FIN_ENGINES))
    if total:
        g.wait_ge(sem.sent, total)
    g.wait_ge(sem.stored, 16 * MB)
